import numpy as np
CORES = [6,14,22,30,38,46,54,62,134,142,150,158,166,174,182,190,262,270,278,286,294,302,310,318,390,398,406,414,422,430,438,446]
N = 32
ROOT = 20
def setup_inputs(rng):
    return {"x": rng.standard_normal((N, 128, N * 4), dtype=np.float32)}
def reference(x):
    return {"y": np.stack([x[ROOT][:, r * 4:(r + 1) * 4] for r in range(N)])}

from concourse.bass import DstId, RemoteDMATransfer

W = 4
HALF = 16
CUTTERS = [2, 3, 7, 6]

SCRATCH = {
    "td": ("dram", [7, 128, 16], "float32"),
    "pd": ("dram", [16, 128, 1], "float32"),
    "ld": ("dram", [4, 128, 1], "float32"),
}
SEMAPHORES = [
    "split_far", "split_near",
    "tile",
    "cut_a", "cut_b",
    "mine",
    "read",
    "arrived",
    "stored",
]


def _transfer(topo, core, dst_core, mask, sem, src, dst):
    rid, pid = topo.addr(dst_core, core)
    return RemoteDMATransfer(dst_ids=[DstId(rid=rid, pnc=pid)], dma_engine_mask=mask, remote_sem=sem, src=src, dst=dst)


def _cut_and_send(g, core, T, topo, h, base, block_of):
    queues = [g.sync, g.scalar]
    other = [j for j in range(HALF) if T.cores[base + j] != core and base + j != T.root]
    halves = [(other[:8], T.sem.cut_a), (other[8:], T.sem.cut_b)]
    n = 0
    for js, sem in halves:
        for j in js:
            queues[n % 2].dma_start(T.pd[j], block_of(j)).then_inc(sem, 16)
            n += 1
    own = T.rank_of(core) is not None and core != T.cores[T.root]
    if own:
        queues[n % 2].dma_start(T.ld[h], block_of(T.rank_of(core) - base)).then_inc(T.sem.mine, 16)
    sent = 0
    for js, sem in halves:
        g.wait_ge(sem, 16 * len(js))
        g.remote_dma_fused([_transfer(topo, core, T.cores[base + j], 1 << e, T.sem.arrived, T.pd[j], T.ld[h])
                            for e, j in enumerate(js)], local_sem=T.sem.read)
        sent += len(js)
    return sent, own


def rank_program(g, core, T, topo):
    rank = T.rank_of(core)
    root = T.cores[T.root]
    chip0 = root - root % 8
    far0 = (3 - topo.host(root)) * 128 + chip0 % 128
    near_base = HALF * topo.rack(topo.host(root))
    far_base = HALF - near_base

    if core == root:
        fc, nc = far_base * W, near_base * W
        g.sync.dma_start(T.td[0:4], T.x[:, fc:fc + 64]).then_inc(T.sem.split_far, 16)
        g.scalar.dma_start(T.td[4:7], T.x[0:96, nc:nc + 64]).then_inc(T.sem.split_near, 16)
        g.wait_ge(T.sem.split_far, 16)
        g.remote_dma_fused([_transfer(topo, core, far0 + CUTTERS[h], 3 << (2 * h), T.sem.tile, T.td[h], T.td[0])
                            for h in range(4)], local_sem=T.sem.read)
        g.wait_ge(T.sem.split_near, 16)
        g.remote_dma_fused([_transfer(topo, core, chip0 + CUTTERS[h], 3 << (8 + 2 * h), T.sem.tile, T.td[4 + h], T.td[0])
                            for h in range(3)], local_sem=T.sem.read)
        sent, _ = _cut_and_send(g, core, T, topo, 3, near_base,
                                lambda j: T.x[96:128, nc + W * j:nc + W * (j + 1)])
        g.sync.dma_start(T.y[:], T.x[:, rank * W:(rank + 1) * W]).then_inc(T.sem.stored, 16)
        g.wait_ge(T.sem.read, 8 + 6 + sent)
        g.wait_ge(T.sem.stored, 16)
        return

    if core - core % 8 in (chip0, far0) and core % 8 in CUTTERS:
        h = CUTTERS.index(core % 8)
        base = near_base if core - core % 8 == chip0 else far_base
        g.sync.wait_ge(T.sem.tile, 2)
        g.scalar.wait_ge(T.sem.tile, 2)
        sent, own = _cut_and_send(g, core, T, topo, h, base,
                                  lambda j: T.td[0, (j // 4)::4, W * (j % 4):W * (j % 4 + 1)])
        if own:
            g.sync.wait_ge(T.sem.mine, 16)
            g.sync.wait_ge(T.sem.arrived, 3)
            g.sync.dma_start(T.y[:], T.ld[:]).then_inc(T.sem.stored, 16)
            g.wait_ge(T.sem.stored, 16)
        g.wait_ge(T.sem.read, sent)
        return

    if rank is None:
        return
    g.sync.wait_ge(T.sem.arrived, 4)
    g.sync.dma_start(T.y[:], T.ld[:]).then_inc(T.sem.stored, 16)
    g.wait_ge(T.sem.stored, 16)
